import numpy as np
import ml_dtypes


def mxq(x, axis, fmt="e4m3"):
    dtype, down = {"e4m3": (ml_dtypes.float8_e4m3fn, 7), "e5m2": (ml_dtypes.float8_e5m2, 14)}[fmt]
    v = np.moveaxis(np.asarray(x, np.float32).astype(ml_dtypes.bfloat16).astype(np.float64), axis, -1)
    blocks = v.reshape(v.shape[:-1] + (-1, 32))
    amax = np.abs(blocks).max(-1, keepdims=True)
    byte = np.maximum(np.where(amax > 0, np.frexp(amax)[1] - 1 + 127, 0) - down, 1)
    scale = np.exp2(byte - 127.0)
    codes = (blocks / scale).astype(np.float32).astype(dtype).astype(np.float64)
    return np.moveaxis((codes * scale).reshape(v.shape), -1, axis)


WIDE = False


def mx_kscale(k):
    if not WIDE:
        return np.ones(k)
    levels = np.array([10, -10, 5, -5, 0])
    if k % 512:
        return np.exp2(np.random.permutation(np.resize(levels, k // 32))).repeat(32)
    a = np.empty((k // 512, 16))
    for p in range(k // 512):
        a[p, :8] = np.random.permutation(np.resize(levels, 8))
        for g in range(8):
            far = levels[np.abs(levels - a[p, g]) >= 10]
            a[p, g + 8] = far[np.random.randint(len(far))]
    return np.exp2(a.ravel()).repeat(32)


def f64(x):
    return np.asarray(x).astype(np.float64)


def striped(idx):
    return np.tile(idx.reshape(-1, 16).T, (8, 1)).astype(np.uint16)


def unstriped(offs):
    return offs[:16].T.reshape(-1).astype(np.int64)


def striped8(idx):
    return np.concatenate([x.reshape(-1, 16).T for x in idx]).astype(np.uint16)


def runs(offs, k):
    lists = np.stack([offs[16 * r : 16 * r + 16].T.reshape(-1) for r in range(8)]).astype(np.int64)
    return lists[np.arange(k) % 512 // 64]


def pack_weight(w):
    k, n = w.shape
    w = f64(np.asarray(w, np.float32).astype(ml_dtypes.bfloat16)).reshape(k // 32, 32, n)
    amax = np.abs(w).max(1)
    byte = np.clip(np.where(amax > 0, np.frexp(amax)[1] - 1 + 127 - 7, 1), 1, 254)
    scaled = (w * np.exp2(127.0 - byte)[:, None, :]).reshape(k, n).astype(np.float32)
    words = np.ascontiguousarray(scaled.reshape(k // 512, 128, 4, n).transpose(0, 1, 3, 2)).astype(ml_dtypes.float8_e4m3fn).view(np.uint8)
    return words, np.ascontiguousarray(byte.astype(np.uint8).reshape(k // 512, 16, n))


def unpack_weight(words, scales):
    g, p, n, _ = words.shape
    vals = np.ascontiguousarray(words).view(ml_dtypes.float8_e4m3fn).astype(np.float64) * np.repeat(np.exp2(scales.astype(np.float64) - 127.0), 8, axis=1)[..., None]
    return vals.transpose(0, 1, 3, 2).reshape(g * 512, n)


K, T, S, H, C = 512, 2048, 512, 512, 512


def setup_inputs():
    n = np.random.standard_normal
    s = mx_kscale(K)[:, None]
    packed_xT = pack_weight(n((K, T)) * s)
    return {
        "x_words": packed_xT[0],
        "x_scales": packed_xT[1],
        "w1": (n((K, H)) / np.sqrt(K) / s).astype(np.float32),
        "gs": (np.random.uniform(0.5, 1.5, (K, 1)) / s).astype(np.float32),
        "offs": striped(np.random.permutation(T)[:S]),
        "n1": striped8(np.stack([np.random.permutation(S) for _ in range(8)])),
        "n2": striped8(np.stack([np.random.permutation(S) for _ in range(8)])),
        "ca": striped(np.random.permutation(T)[:C]),
        "cb": striped(np.random.permutation(T)[:C]),
        "n3": striped8(np.stack([np.random.permutation(S) for _ in range(8)])),
        "n4": striped8(np.stack([np.random.permutation(S) for _ in range(8)])),
    }


def reference(x_words, x_scales, w1, gs, offs, n1, n2, ca, cb, n3, n4):
    x_ca = unpack_weight(x_words, x_scales)[:, unstriped(ca)]
    xq = unpack_weight(x_words, x_scales)[:, unstriped(offs)]
    y = mxq(f64(w1), 0, "e4m3").T @ xq
    st = np.maximum(y, y[np.arange(H)[:, None], runs(n1, H)])
    z = f64(gs) * (np.minimum(st, st[np.arange(H)[:, None], runs(n2, H)]))
    zq = mxq(z, 0, "e4m3")
    a = 0.0625 * (x_ca.T @ zq)
    x_cb = unpack_weight(x_words, x_scales)[:, unstriped(cb)]
    b = 0.0625 * (x_cb.T @ zq)
    return np.maximum(a, b[np.arange(C)[:, None], runs(n4, C)]) - (np.minimum(a[np.arange(C)[:, None], runs(n3, C)], b))

@@ -1,0 +1,204 @@
+from contextlib import ExitStack
+
+import concourse.mybir as mybir
+
+K, T, S = 512, 2048, 512
+P = 128
+PACK = 4
+FLOPS = 3 * 2 * K * S * S
+
+F32 = mybir.dt.float32
+BF16 = mybir.dt.bfloat16
+I32 = mybir.dt.int32
+U32 = mybir.dt.uint32
+U16 = mybir.dt.uint16
+U8 = mybir.dt.uint8
+FP8X4 = mybir.dt.float8_e4m3fn_x4
+ALU = mybir.AluOpType
+COPY = mybir.ActivationFunctionType.Copy
+
+
+def tile_picked_ccmpmaxbhopmn_none_p_kernel(
+    tc, x_words, x_scales, w1, gs, offs, n1, n2, ca, cb, n3, n4, out
+):
+    nc = tc.nc
+    with ExitStack() as ctx:
+        lists = ctx.enter_context(tc.tile_pool(name="lists", bufs=1))
+        keep = ctx.enter_context(tc.tile_pool(name="keep", bufs=1))
+        work = ctx.enter_context(tc.tile_pool(name="work", bufs=2))
+        psum = ctx.enter_context(tc.psum_pool(name="psum", bufs=8))
+
+        table_scales = keep.tile([P, T], U8, name="table_scales", align_bytes=64)
+        nc.vector.memset(table_scales[:].bitcast(I32), 0)
+
+        table_words = keep.tile([P, T], I32, name="table_words", align_bytes=64)
+        nc.scalar.dma_start(out=table_words[:], in_=x_words[0].rearrange("p n t -> p (n t)").bitcast(I32))
+
+        def load_list(src, name):
+            dst = lists.tile([P, S // 16], U16, name=name)
+            nc.sync.dma_start(dst[:], src)
+            return dst
+
+        offs_sb = load_list(offs, "offs_sb")
+        ca_sb = load_list(ca, "ca_sb")
+        for q in range(4):
+            nc.sync.dma_start(
+                out=table_scales[32 * q : 32 * q + 4, :].bitcast(I32),
+                in_=x_scales[0, 4 * q : 4 * q + 4, :].bitcast(I32),
+            )
+        w_rows = w1.rearrange("(p j) c -> p j c", j=PACK)
+        w_raw = []
+        for h in range(2):
+            half = keep.tile([P, PACK, S // 2], F32, name=f"w_raw{h}")
+            nc.scalar.dma_start(out=half[:], in_=w_rows[:, :, h * (S // 2) : (h + 1) * (S // 2)])
+            w_raw.append(half)
+        n1_sb = load_list(n1, "n1_sb")
+        n2_sb = load_list(n2, "n2_sb")
+        gain = keep.tile([P, PACK], F32, name="gain")
+        nc.sync.dma_start(out=gain[:], in_=gs.rearrange("(p t) o -> p (t o)", t=PACK))
+        cb_sb = load_list(cb, "cb_sb")
+        n3_sb = load_list(n3, "n3_sb")
+        n4_sb = load_list(n4, "n4_sb")
+
+        first = [keep.tile([P, 2 * S], F32, name=f"first{t}") for t in range(PACK)]
+        second = [keep.tile([P, 2 * S], F32, name=f"second{t}") for t in range(PACK)]
+        for t in range(PACK):
+            nc.vector.memset(first[t][:, S:], 0.0)
+
+        words_window = table_words[:].bitcast(U32)
+
+        xq_words = keep.tile([P, S], U32, name="xq_words", align_bytes=64)
+        xq_scales = keep.tile([P, S], U8, name="xq_scales", align_bytes=64)
+        nc.vector.tensor_copy(xq_words[:], words_window.indirect(offs_sb[:]))
+        nc.vector.tensor_copy(xq_scales[:], table_scales[:].indirect(offs_sb[:]))
+
+        w_grouped = keep.tile([P, PACK * S], BF16, name="w_grouped", align_bytes=64)
+        w_view = w_grouped[:].rearrange("p (t m j) -> p m j t", t=PACK, j=PACK)
+        for h in range(2):
+            nc.scalar.copy(
+                out=w_view[:, h * 64 : (h + 1) * 64, :, :],
+                in_=w_raw[h][:].rearrange("p j (m t) -> p m j t", t=PACK),
+            )
+        w_words = keep.tile([P, S], U32, name="w_words", align_bytes=64)
+        w_scales = keep.tile([P, S], U8, name="w_scales", align_bytes=64)
+        nc.vector.quantize_mx(out=w_words[:].bitcast(FP8X4), scales=w_scales[:], in_=w_grouped[:])
+
+        def gather_words(index_sb, name, tag):
+            words = keep.tile([P, S], U32, name=name, tag=tag, align_bytes=64)
+            nc.vector.tensor_copy(words[:].rearrange("p (t m) -> p m t", t=PACK), words_window.indirect(index_sb[:]))
+            return words
+
+        def gather_scales(index_sb, name, tag):
+            listed = keep.tile([P, S], U8, name=name + "_listed", tag=tag, align_bytes=64)
+            nc.vector.tensor_copy(listed[:], table_scales[:].indirect(index_sb[:]))
+            dealt = keep.tile([P, S], U8, name=name, align_bytes=64)
+            nc.vector.tensor_copy(
+                dealt[:].rearrange("p (t m) -> p t m", t=PACK), listed[:].rearrange("p (m t) -> p t m", t=PACK)
+            )
+            return dealt
+
+        ca_words = gather_words(ca_sb, "ca_words", "ca_words")
+        ca_scales = gather_scales(ca_sb, "ca_scales", "ca_listed")
+
+        def product(lhs_words, lhs_scales, t, rhs_words, rhs_scales, dst, scale):
+            cols = slice(t * P, (t + 1) * P)
+            acc = psum.tile([P, S], F32, name="acc")
+            nc.tensor.matmul_mx(
+                out=acc[:],
+                lhsT=lhs_words[:, cols].bitcast(FP8X4),
+                lhsT_scale=lhs_scales[:, cols],
+                rhs=rhs_words[:].bitcast(FP8X4),
+                rhs_scale=rhs_scales[:],
+                start=True,
+                stop=True,
+            )
+            nc.scalar.activation(out=dst, in_=acc[:], func=COPY, scale=scale)
+
+        for t in range(PACK):
+            product(w_words, w_scales, t, xq_words, xq_scales, first[t][:, :S], 1.0)
+
+        z_grouped = keep.tile([P, PACK * S], BF16, name="z_grouped", tag="z_then_cb", align_bytes=64)
+        z_view = z_grouped[:].rearrange("p (c t) -> p c t", t=PACK)
+        hop2 = {}
+
+        def fetch1(t):
+            nc.vector.tensor_copy(second[t][:, S:], first[t][:].indirect(n1_sb[:]))
+
+        def larger(t):
+            nc.vector.tensor_tensor(second[t][:, :S], first[t][:, :S], second[t][:, S:], ALU.max)
+
+        def fetch2(t):
+            if t == PACK - 1:
+                hop2[t] = keep.tile([P, S], F32, name="hop2_last", tag="last_then_cb", align_bytes=64)
+            else:
+                hop2[t] = work.tile([P, S], F32, name="hop2")
+            nc.vector.tensor_copy(hop2[t][:], second[t][:].indirect(n2_sb[:]))
+
+        def smaller(t):
+            low = work.tile([P, S], F32, name="low")
+            nc.vector.tensor_tensor(low[:], second[t][:, :S], hop2[t][:], ALU.min)
+            nc.scalar.activation(out=z_view[:, :, t], in_=low[:], func=COPY, scale=gain[:, t : t + 1])
+
+        fetch1(0)
+        fetch1(1)
+        larger(0)
+        larger(1)
+        fetch2(0)
+        fetch1(2)
+        smaller(0)
+        fetch2(1)
+        larger(2)
+        fetch1(3)
+        smaller(1)
+        fetch2(2)
+        larger(3)
+        smaller(2)
+        fetch2(3)
+        smaller(3)
+
+        cb_scales = gather_scales(cb_sb, "cb_scales", "last_then_cb")
+        z_words = keep.tile([P, S], U32, name="z_words", align_bytes=64)
+        z_scales = keep.tile([P, S], U8, name="z_scales", align_bytes=64)
+        nc.vector.quantize_mx(out=z_words[:].bitcast(FP8X4), scales=z_scales[:], in_=z_grouped[:])
+        cb_words = gather_words(cb_sb, "cb_words", "z_then_cb")
+
+        product(ca_words, ca_scales, 0, z_words, z_scales, first[0][:, :S], 0.0625)
+        product(ca_words, ca_scales, 1, z_words, z_scales, first[1][:, :S], 0.0625)
+        for t in range(PACK):
+            product(cb_words, cb_scales, t, z_words, z_scales, second[t][:, :S], 0.0625)
+            if t + 2 < PACK:
+                product(ca_words, ca_scales, t + 2, z_words, z_scales, first[t + 2][:, :S], 0.0625)
+
+        out_rows = out.rearrange("(p t) j -> p t j", t=PACK)
+        a3, b4, hi, lo = {}, {}, {}, {}
+
+        def fetch3(t):
+            a3[t] = work.tile([P, S], F32, name="a3", bufs=3)
+            nc.vector.tensor_copy(a3[t][:], first[t][:].indirect(n3_sb[:]))
+
+        def fetch4(t):
+            b4[t] = work.tile([P, S], F32, name="b4")
+            nc.vector.tensor_copy(b4[t][:], second[t][:].indirect(n4_sb[:]))
+
+        def low_side(t):
+            lo[t] = work.tile([P, S], F32, name="lo")
+            nc.vector.tensor_tensor(lo[t][:], a3[t][:], second[t][:, :S], ALU.min)
+
+        def high_side(t):
+            hi[t] = work.tile([P, S], F32, name="hi")
+            nc.vector.tensor_tensor(hi[t][:], first[t][:, :S], b4[t][:], ALU.max)
+
+        def finish(t):
+            res = work.tile([P, S], F32, name="res", bufs=4)
+            nc.vector.tensor_tensor(res[:], hi[t][:], lo[t][:], ALU.subtract)
+            nc.sync.dma_start(out=out_rows[:, t, :], in_=res[:])
+
+        fetch3(0)
+        fetch3(1)
+        for t in range(PACK):
+            fetch4(t)
+            low_side(t)
+            high_side(t)
+            if t + 2 < PACK:
+                fetch3(t + 2)
+            finish(t)

@@ -1,6 +1,7 @@
 from contextlib import ExitStack
 
 import concourse.mybir as mybir
+from concourse.masks import make_identity
 
 K, T, S = 512, 2048, 512
 P = 128
@@ -16,6 +17,7 @@ U8 = mybir.dt.uint8
 FP8X4 = mybir.dt.float8_e4m3fn_x4
 ALU = mybir.AluOpType
 COPY = mybir.ActivationFunctionType.Copy
+RELU = mybir.ActivationFunctionType.Relu
 
 
 def tile_picked_ccmpmaxbhopmn_none_p_kernel(
@@ -26,7 +28,8 @@ def tile_picked_ccmpmaxbhopmn_none_p_kernel(
         lists = ctx.enter_context(tc.tile_pool(name="lists", bufs=1))
         keep = ctx.enter_context(tc.tile_pool(name="keep", bufs=1))
         work = ctx.enter_context(tc.tile_pool(name="work", bufs=2))
-        psum = ctx.enter_context(tc.psum_pool(name="psum", bufs=8))
+        psum = ctx.enter_context(tc.psum_pool(name="psum", bufs=4))
+        psum_sum = ctx.enter_context(tc.psum_pool(name="psum_sum", bufs=2))
 
         table_scales = keep.tile([P, T], U8, name="table_scales", align_bytes=64)
         nc.vector.memset(table_scales[:].bitcast(I32), 0)
@@ -65,6 +68,9 @@ def tile_picked_ccmpmaxbhopmn_none_p_kernel(
         for t in range(PACK):
             nc.vector.memset(first[t][:, S:], 0.0)
 
+        identity = keep.tile([P, P], F32, name="identity")
+        make_identity(nc, identity[:])
+
         words_window = table_words[:].bitcast(U32)
 
         xq_words = keep.tile([P, S], U32, name="xq_words", align_bytes=64)
@@ -72,7 +78,7 @@ def tile_picked_ccmpmaxbhopmn_none_p_kernel(
         nc.vector.tensor_copy(xq_words[:], words_window.indirect(offs_sb[:]))
         nc.vector.tensor_copy(xq_scales[:], table_scales[:].indirect(offs_sb[:]))
 
-        w_grouped = keep.tile([P, PACK * S], BF16, name="w_grouped", align_bytes=64)
+        w_grouped = keep.tile([P, PACK * S], BF16, name="w_grouped", tag="w_then_ca", align_bytes=64)
         w_view = w_grouped[:].rearrange("p (t m j) -> p m j t", t=PACK, j=PACK)
         for h in range(2):
             nc.scalar.copy(
@@ -98,7 +104,7 @@ def tile_picked_ccmpmaxbhopmn_none_p_kernel(
             return dealt
 
         ca_words = gather_words(ca_sb, "ca_words", "ca_words")
-        ca_scales = gather_scales(ca_sb, "ca_scales", "ca_listed")
+        ca_scales = gather_scales(ca_sb, "ca_scales", "w_then_ca")
 
         def product(lhs_words, lhs_scales, t, rhs_words, rhs_scales, dst, scale):
             cols = slice(t * P, (t + 1) * P)
@@ -165,40 +171,77 @@ def tile_picked_ccmpmaxbhopmn_none_p_kernel(
         product(ca_words, ca_scales, 0, z_words, z_scales, first[0][:, :S], 0.0625)
         product(ca_words, ca_scales, 1, z_words, z_scales, first[1][:, :S], 0.0625)
         for t in range(PACK):
-            product(cb_words, cb_scales, t, z_words, z_scales, second[t][:, :S], 0.0625)
+            product(cb_words, cb_scales, t, z_words, z_scales, second[t][:, :S], -0.0625)
             if t + 2 < PACK:
                 product(ca_words, ca_scales, t + 2, z_words, z_scales, first[t + 2][:, :S], 0.0625)
 
         out_rows = out.rearrange("(p t) j -> p t j", t=PACK)
-        a3, b4, hi, lo = {}, {}, {}, {}
+        a3, neg_low, diff = {}, {}, {}
+        last = PACK - 1
 
         def fetch3(t):
-            a3[t] = work.tile([P, S], F32, name="a3", bufs=3)
+            a3[t] = work.tile([P, S], F32, name="a3", tag=f"a3_{min(t, last - 1)}", bufs=1)
             nc.vector.tensor_copy(a3[t][:], first[t][:].indirect(n3_sb[:]))
 
-        def fetch4(t):
-            b4[t] = work.tile([P, S], F32, name="b4")
-            nc.vector.tensor_copy(b4[t][:], second[t][:].indirect(n4_sb[:]))
-
         def low_side(t):
-            lo[t] = work.tile([P, S], F32, name="lo")
-            nc.vector.tensor_tensor(lo[t][:], a3[t][:], second[t][:, :S], ALU.min)
+            neg_low[t] = work.tile([P, S], F32, name="neg_low", bufs=4)
+            nc.vector.scalar_tensor_tensor(neg_low[t][:], a3[t][:], -1.0, second[t][:, :S], ALU.mult, ALU.max)
 
-        def high_side(t):
-            hi[t] = work.tile([P, S], F32, name="hi")
-            nc.vector.tensor_tensor(hi[t][:], first[t][:, :S], b4[t][:], ALU.max)
+        def fetch4(t):
+            diff[t] = work.tile([P, S], F32, name="diff", bufs=3)
+            nc.vector.tensor_tensor(diff[t][:], second[t][:].indirect(n4_sb[:]), first[t][:, :S], ALU.add)
 
-        def finish(t):
-            res = work.tile([P, S], F32, name="res", bufs=4)
-            nc.vector.tensor_tensor(res[:], hi[t][:], lo[t][:], ALU.subtract)
+        def sum_on_tensor(t):
+            excess = work.tile([P, S], F32, name="excess", bufs=1)
+            nc.scalar.activation(out=excess[:], in_=diff[t][:], func=RELU, scale=-1.0)
+            turned = psum_sum.tile([P, S], F32, name="turned", bufs=1)
+            terms = [first[t], excess, neg_low[t]]
+            for n, term in enumerate(terms):
+                for c in range(PACK):
+                    cols = slice(c * P, (c + 1) * P)
+                    nc.tensor.matmul(
+                        turned[:, cols],
+                        term[:, cols],
+                        identity[:],
+                        is_transpose=True,
+                        start=(n == 0 and c == 0),
+                        stop=(n == len(terms) - 1 and c == PACK - 1),
+                    )
+            turned_sb = work.tile([P, S], F32, name="turned_sb")
+            nc.scalar.copy(out=turned_sb[:], in_=turned[:])
+            back = psum_sum.tile([P, S], F32, name="back")
+            for c in range(PACK):
+                cols = slice(c * P, (c + 1) * P)
+                nc.tensor.transpose(back[:, cols], turned_sb[:, cols], identity[:])
+            res = work.tile([P, S], F32, name="res", bufs=3)
+            nc.scalar.copy(out=res[:], in_=back[:])
             nc.sync.dma_start(out=out_rows[:, t, :], in_=res[:])
+
+        halves = [slice(h * (S // 2), (h + 1) * (S // 2)) for h in range(2)]
+        neg_b4 = [work.tile([P, S // 2], F32, name="neg_b4") for h in range(2)]
+        high = [work.tile([P, S // 2], F32, name="high") for h in range(2)]
+
+        def fetch4_last(h):
+            nc.vector.tensor_copy(neg_b4[h][:], second[last][:].indirect(n4_sb[:, h * 16 : (h + 1) * 16]))
 
         fetch3(0)
         fetch3(1)
-        for t in range(PACK):
+        fetch4(0)
+        low_side(0)
+        for t in range(1, last):
             fetch4(t)
+            if t + 1 < last:
+                fetch3(t + 1)
             low_side(t)
-            high_side(t)
-            if t + 2 < PACK:
-                fetch3(t + 2)
-            finish(t)
+        for t in range(last):
+            sum_on_tensor(t)
+        fetch3(last)
+        fetch4_last(0)
+        low_side(last)
+        fetch4_last(1)
+        for h in range(2):
+            nc.vector.scalar_tensor_tensor(high[h][:], neg_b4[h][:], -1.0, first[last][:, halves[h]], ALU.mult, ALU.max)
+        for h in range(2):
+            res = work.tile([P, S // 2], F32, name="res_half")
+            nc.vector.tensor_tensor(res[:], high[h][:], neg_low[last][:, halves[h]], ALU.add)
+            nc.sync.dma_start(out=out_rows[:, last, halves[h]], in_=res[:])

@@ -168,35 +168,45 @@ def tile_picked_ccmpmaxbhopmn_none_p_kernel(
         nc.vector.quantize_mx(out=z_words[:].bitcast(FP8X4), scales=z_scales[:], in_=z_grouped[:])
         cb_words = gather_words(cb_sb, "cb_words", "z_then_cb")
 
-        product(ca_words, ca_scales, 0, z_words, z_scales, first[0][:, :S], 0.0625)
-        product(ca_words, ca_scales, 1, z_words, z_scales, first[1][:, :S], 0.0625)
-        for t in range(PACK):
-            product(cb_words, cb_scales, t, z_words, z_scales, second[t][:, :S], -0.0625)
-            if t + 2 < PACK:
-                product(ca_words, ca_scales, t + 2, z_words, z_scales, first[t + 2][:, :S], 0.0625)
-
         out_rows = out.rearrange("(p t) j -> p t j", t=PACK)
-        a3, neg_low, diff = {}, {}, {}
-        last = PACK - 1
+        on_tensor, on_vector = (0, 1), (2, 3)
+
+        def score_a(t):
+            product(ca_words, ca_scales, t, z_words, z_scales, first[t][:, :S], 0.0625)
+
+        def score_neg_b(t):
+            product(cb_words, cb_scales, t, z_words, z_scales, second[t][:, :S], -0.0625)
+
+        score_a(2)
+        for t in on_tensor:
+            score_a(t)
+            score_neg_b(t)
+        score_neg_b(2)
+        score_a(3)
+        score_neg_b(3)
+
+        a3, neg_b4, neg_low, high = {}, {}, {}, {}
 
         def fetch3(t):
-            a3[t] = work.tile([P, S], F32, name="a3", tag=f"a3_{min(t, last - 1)}", bufs=1)
+            a3[t] = work.tile([P, S], F32, name="a3")
             nc.vector.tensor_copy(a3[t][:], first[t][:].indirect(n3_sb[:]))
 
-        def low_side(t):
-            neg_low[t] = work.tile([P, S], F32, name="neg_low", bufs=4)
-            nc.vector.scalar_tensor_tensor(neg_low[t][:], a3[t][:], -1.0, second[t][:, :S], ALU.mult, ALU.max)
+        fetch3(2)
 
-        def fetch4(t):
-            diff[t] = work.tile([P, S], F32, name="diff", bufs=3)
-            nc.vector.tensor_tensor(diff[t][:], second[t][:].indirect(n4_sb[:]), first[t][:, :S], ALU.add)
+        excess = {}
+        for t in on_tensor:
+            a, neg_b = first[t][:, :S], second[t][:, :S]
+            for side, (window, index_sb, other) in enumerate([(second[t], n4_sb, a), (first[t], n3_sb, neg_b)]):
+                diff = work.tile([P, S], F32, name="diff", bufs=4)
+                nc.vector.tensor_tensor(diff[:], window[:].indirect(index_sb[:]), other, ALU.add)
+                excess[t, side] = work.tile([P, S], F32, name="excess", bufs=4)
+                nc.scalar.activation(out=excess[t, side][:], in_=diff[:], func=RELU, scale=-1.0)
 
-        def sum_on_tensor(t):
-            excess = work.tile([P, S], F32, name="excess", bufs=1)
-            nc.scalar.activation(out=excess[:], in_=diff[t][:], func=RELU, scale=-1.0)
-            turned = psum_sum.tile([P, S], F32, name="turned", bufs=1)
-            terms = [first[t], excess, neg_low[t]]
-            for n, term in enumerate(terms):
+        turned_sb = {}
+        for t in on_tensor:
+            turned = psum_sum.tile([P, S], F32, name="turned")
+            addends = [first[t][:, :S], second[t][:, :S], excess[t, 0][:], excess[t, 1][:]]
+            for n, term in enumerate(addends):
                 for c in range(PACK):
                     cols = slice(c * P, (c + 1) * P)
                     nc.tensor.matmul(
@@ -205,43 +215,51 @@ def tile_picked_ccmpmaxbhopmn_none_p_kernel(
                         identity[:],
                         is_transpose=True,
                         start=(n == 0 and c == 0),
-                        stop=(n == len(terms) - 1 and c == PACK - 1),
+                        stop=(n == len(addends) - 1 and c == PACK - 1),
                     )
-            turned_sb = work.tile([P, S], F32, name="turned_sb")
-            nc.scalar.copy(out=turned_sb[:], in_=turned[:])
+            turned_sb[t] = work.tile([P, S], F32, name="turned_sb")
+            nc.scalar.copy(out=turned_sb[t][:], in_=turned[:])
+        for t in on_tensor:
             back = psum_sum.tile([P, S], F32, name="back")
             for c in range(PACK):
                 cols = slice(c * P, (c + 1) * P)
-                nc.tensor.transpose(back[:, cols], turned_sb[:, cols], identity[:])
+                nc.tensor.transpose(back[:, cols], turned_sb[t][:, cols], identity[:])
             res = work.tile([P, S], F32, name="res", bufs=3)
             nc.scalar.copy(out=res[:], in_=back[:])
-            nc.sync.dma_start(out=out_rows[:, t, :], in_=res[:])
+            nc.scalar.dma_start(out=out_rows[:, t, :], in_=res[:])
 
+        def fetch4(t, cols):
+            offsets = n4_sb[:, cols.start // 16 : cols.stop // 16]
+            nc.vector.tensor_copy(neg_b4[t][:, cols], second[t][:].indirect(offsets))
+
+        def low_side(t):
+            nc.vector.scalar_tensor_tensor(neg_low[t][:], a3[t][:], -1.0, second[t][:, :S], ALU.mult, ALU.max)
+
+        def high_side(t, cols):
+            nc.vector.scalar_tensor_tensor(
+                high[t][:, cols], neg_b4[t][:, cols], -1.0, first[t][:, cols], ALU.mult, ALU.max
+            )
+
+        def finish(t, cols):
+            res = work.tile([P, cols.stop - cols.start], F32, name="res_v", bufs=3)
+            nc.vector.tensor_tensor(res[:], high[t][:, cols], neg_low[t][:, cols], ALU.add)
+            nc.sync.dma_start(out=out_rows[:, t, cols], in_=res[:])
+
+        for t in on_vector:
+            neg_b4[t] = work.tile([P, S], F32, name="neg_b4")
+            neg_low[t] = work.tile([P, S], F32, name="neg_low")
+            high[t] = work.tile([P, S], F32, name="high")
+        whole = slice(0, S)
         halves = [slice(h * (S // 2), (h + 1) * (S // 2)) for h in range(2)]
-        neg_b4 = [work.tile([P, S // 2], F32, name="neg_b4") for h in range(2)]
-        high = [work.tile([P, S // 2], F32, name="high") for h in range(2)]
-
-        def fetch4_last(h):
-            nc.vector.tensor_copy(neg_b4[h][:], second[last][:].indirect(n4_sb[:, h * 16 : (h + 1) * 16]))
-
-        fetch3(0)
-        fetch3(1)
-        fetch4(0)
-        low_side(0)
-        for t in range(1, last):
-            fetch4(t)
-            if t + 1 < last:
-                fetch3(t + 1)
-            low_side(t)
-        for t in range(last):
-            sum_on_tensor(t)
-        fetch3(last)
-        fetch4_last(0)
-        low_side(last)
-        fetch4_last(1)
-        for h in range(2):
-            nc.vector.scalar_tensor_tensor(high[h][:], neg_b4[h][:], -1.0, first[last][:, halves[h]], ALU.mult, ALU.max)
-        for h in range(2):
-            res = work.tile([P, S // 2], F32, name="res_half")
-            nc.vector.tensor_tensor(res[:], high[h][:], neg_low[last][:, halves[h]], ALU.add)
-            nc.sync.dma_start(out=out_rows[:, last, halves[h]], in_=res[:])
+        fetch4(2, whole)
+        low_side(2)
+        high_side(2, whole)
+        fetch3(3)
+        finish(2, whole)
+        fetch4(3, halves[0])
+        low_side(3)
+        fetch4(3, halves[1])
+        for cols in halves:
+            high_side(3, cols)
+        for cols in halves:
+            finish(3, cols)

@@ -58,7 +58,7 @@ def tile_picked_ccmpmaxbhopmn_none_p_kernel(
         n1_sb = load_list(n1, "n1_sb")
         n2_sb = load_list(n2, "n2_sb")
         gain = keep.tile([P, PACK], F32, name="gain")
-        nc.sync.dma_start(out=gain[:], in_=gs.rearrange("(p t) o -> p (t o)", t=PACK))
+        nc.gpsimd.dma_start(out=gain[:], in_=gs.rearrange("(p t) o -> p (t o)", t=PACK))
         cb_sb = load_list(cb, "cb_sb")
         n3_sb = load_list(n3, "n3_sb")
         n4_sb = load_list(n4, "n4_sb")
@@ -91,7 +91,7 @@ def tile_picked_ccmpmaxbhopmn_none_p_kernel(
 
         def gather_words(index_sb, name, tag):
             words = keep.tile([P, S], U32, name=name, tag=tag, align_bytes=64)
-            nc.vector.tensor_copy(words[:].rearrange("p (t m) -> p m t", t=PACK), words_window.indirect(index_sb[:]))
+            nc.vector.tensor_copy(words[:].rearrange("p (t h c) -> p h t c", t=PACK, c=PACK), words_window.indirect(index_sb[:]))
             return words
 
         def gather_scales(index_sb, name, tag):
@@ -99,7 +99,8 @@ def tile_picked_ccmpmaxbhopmn_none_p_kernel(
             nc.vector.tensor_copy(listed[:], table_scales[:].indirect(index_sb[:]))
             dealt = keep.tile([P, S], U8, name=name, align_bytes=64)
             nc.vector.tensor_copy(
-                dealt[:].rearrange("p (t m) -> p t m", t=PACK), listed[:].rearrange("p (m t) -> p t m", t=PACK)
+                dealt[:].bitcast(I32).rearrange("p (t h) -> p t h", t=PACK),
+                listed[:].bitcast(I32).rearrange("p (h t) -> p t h", t=PACK),
             )
             return dealt
 
@@ -159,8 +160,14 @@ def tile_picked_ccmpmaxbhopmn_none_p_kernel(
         fetch2(2)
         larger(3)
         smaller(2)
-        fetch2(3)
-        smaller(3)
+        hop2_last = keep.tile([P, S], F32, name="hop2_last", tag="last_then_cb", align_bytes=64)
+        low_last = work.tile([P, S], F32, name="low")
+        halves = [slice(h * (S // 2), (h + 1) * (S // 2)) for h in range(2)]
+        for cols in halves:
+            nc.vector.tensor_copy(hop2_last[:, cols], second[3][:].indirect(n2_sb[:, cols.start // 16 : cols.stop // 16]))
+        for cols in halves:
+            nc.vector.tensor_tensor(low_last[:, cols], second[3][:, cols], hop2_last[:, cols], ALU.min)
+            nc.scalar.activation(out=z_view[:, cols, 3], in_=low_last[:, cols], func=COPY, scale=gain[:, 3:4])
 
         cb_scales = gather_scales(cb_sb, "cb_scales", "last_then_cb")
         z_words = keep.tile([P, S], U32, name="z_words", align_bytes=64)
@@ -168,7 +175,7 @@ def tile_picked_ccmpmaxbhopmn_none_p_kernel(
         nc.vector.quantize_mx(out=z_words[:].bitcast(FP8X4), scales=z_scales[:], in_=z_grouped[:])
         cb_words = gather_words(cb_sb, "cb_words", "z_then_cb")
 
-        out_rows = out.rearrange("(p t) j -> p t j", t=PACK)
+        out_rows = out.rearrange("(h t c) j -> t h c j", t=PACK, c=PACK)
         on_tensor, on_vector = (0, 1), (2, 3)
 
         def score_a(t):
@@ -226,7 +233,7 @@ def tile_picked_ccmpmaxbhopmn_none_p_kernel(
                 nc.tensor.transpose(back[:, cols], turned_sb[t][:, cols], identity[:])
             res = work.tile([P, S], F32, name="res", bufs=3)
             nc.scalar.copy(out=res[:], in_=back[:])
-            nc.scalar.dma_start(out=out_rows[:, t, :], in_=res[:])
+            nc.scalar.dma_start(out=out_rows[t], in_=res[:])
 
         def fetch4(t, cols):
             offsets = n4_sb[:, cols.start // 16 : cols.stop // 16]
@@ -243,7 +250,7 @@ def tile_picked_ccmpmaxbhopmn_none_p_kernel(
         def finish(t, cols):
             res = work.tile([P, cols.stop - cols.start], F32, name="res_v", bufs=3)
             nc.vector.tensor_tensor(res[:], high[t][:, cols], neg_low[t][:, cols], ALU.add)
-            nc.sync.dma_start(out=out_rows[:, t, cols], in_=res[:])
+            nc.sync.dma_start(out=out_rows[t][:, :, cols], in_=res[:])
 
         for t in on_vector:
             neg_b4[t] = work.tile([P, S], F32, name="neg_b4")

@@ -6,6 +6,8 @@ from concourse.masks import make_identity
 K, T, S = 512, 2048, 512
 P = 128
 PACK = 4
+LIST_ROWS = 16
+SCORE = 0.0625
 FLOPS = 3 * 2 * K * S * S
 
 F32 = mybir.dt.float32
@@ -18,6 +20,14 @@ FP8X4 = mybir.dt.float8_e4m3fn_x4
 ALU = mybir.AluOpType
 COPY = mybir.ActivationFunctionType.Copy
 RELU = mybir.ActivationFunctionType.Relu
+
+WHOLE = slice(0, S)
+HALVES = (slice(0, S // 2), slice(S // 2, S))
+BLOCKS = tuple(slice(c * P, (c + 1) * P) for c in range(PACK))
+
+
+def entries(list_sb, cols):
+    return list_sb[:, cols.start // LIST_ROWS : cols.stop // LIST_ROWS]
 
 
 def tile_picked_ccmpmaxbhopmn_none_p_kernel(
@@ -38,7 +48,7 @@ def tile_picked_ccmpmaxbhopmn_none_p_kernel(
         nc.scalar.dma_start(out=table_words[:], in_=x_words[0].rearrange("p n t -> p (n t)").bitcast(I32))
 
         def load_list(src, name):
-            dst = lists.tile([P, S // 16], U16, name=name)
+            dst = lists.tile([P, S // LIST_ROWS], U16, name=name)
             nc.sync.dma_start(dst[:], src)
             return dst
 
@@ -51,9 +61,9 @@ def tile_picked_ccmpmaxbhopmn_none_p_kernel(
             )
         w_rows = w1.rearrange("(p j) c -> p j c", j=PACK)
         w_raw = []
-        for h in range(2):
+        for h, cols in enumerate(HALVES):
             half = keep.tile([P, PACK, S // 2], F32, name=f"w_raw{h}")
-            nc.scalar.dma_start(out=half[:], in_=w_rows[:, :, h * (S // 2) : (h + 1) * (S // 2)])
+            nc.scalar.dma_start(out=half[:], in_=w_rows[:, :, cols])
             w_raw.append(half)
         n1_sb = load_list(n1, "n1_sb")
         n2_sb = load_list(n2, "n2_sb")
@@ -63,16 +73,15 @@ def tile_picked_ccmpmaxbhopmn_none_p_kernel(
         n3_sb = load_list(n3, "n3_sb")
         n4_sb = load_list(n4, "n4_sb")
 
-        first = [keep.tile([P, 2 * S], F32, name=f"first{t}") for t in range(PACK)]
-        second = [keep.tile([P, 2 * S], F32, name=f"second{t}") for t in range(PACK)]
+        y_a = [keep.tile([P, 2 * S], F32, name=f"y_a{t}") for t in range(PACK)]
+        st_nb = [keep.tile([P, 2 * S], F32, name=f"st_nb{t}") for t in range(PACK)]
         for t in range(PACK):
-            nc.vector.memset(first[t][:, S:], 0.0)
+            nc.vector.memset(y_a[t][:, S:], 0.0)
 
         identity = keep.tile([P, P], F32, name="identity")
         make_identity(nc, identity[:])
 
         words_window = table_words[:].bitcast(U32)
-
         xq_words = keep.tile([P, S], U32, name="xq_words", align_bytes=64)
         xq_scales = keep.tile([P, S], U8, name="xq_scales", align_bytes=64)
         nc.vector.tensor_copy(xq_words[:], words_window.indirect(offs_sb[:]))
@@ -82,21 +91,31 @@ def tile_picked_ccmpmaxbhopmn_none_p_kernel(
         w_view = w_grouped[:].rearrange("p (t m j) -> p m j t", t=PACK, j=PACK)
         for h in range(2):
             nc.scalar.copy(
-                out=w_view[:, h * 64 : (h + 1) * 64, :, :],
+                out=w_view[:, h * (P // 2) : (h + 1) * (P // 2), :, :],
                 in_=w_raw[h][:].rearrange("p j (m t) -> p m j t", t=PACK),
             )
+
+        def quantize(words, scales, grouped, cols):
+            nc.vector.quantize_mx(
+                out=words[:, cols].bitcast(FP8X4),
+                scales=scales[:, cols],
+                in_=grouped[:, PACK * cols.start : PACK * cols.stop],
+            )
+
         w_words = keep.tile([P, S], U32, name="w_words", align_bytes=64)
         w_scales = keep.tile([P, S], U8, name="w_scales", align_bytes=64)
-        nc.vector.quantize_mx(out=w_words[:].bitcast(FP8X4), scales=w_scales[:], in_=w_grouped[:])
+        for cols in BLOCKS:
+            quantize(w_words, w_scales, w_grouped, cols)
 
-        def gather_words(index_sb, name, tag):
+        def gather_words(list_sb, name, tag):
             words = keep.tile([P, S], U32, name=name, tag=tag, align_bytes=64)
-            nc.vector.tensor_copy(words[:].rearrange("p (t h c) -> p h t c", t=PACK, c=PACK), words_window.indirect(index_sb[:]))
+            dealt_view = words[:].rearrange("p (t h c) -> p h t c", t=PACK, c=PACK)
+            nc.vector.tensor_copy(dealt_view, words_window.indirect(list_sb[:]))
             return words
 
-        def gather_scales(index_sb, name, tag):
+        def gather_scales(list_sb, name, tag):
             listed = keep.tile([P, S], U8, name=name + "_listed", tag=tag, align_bytes=64)
-            nc.vector.tensor_copy(listed[:], table_scales[:].indirect(index_sb[:]))
+            nc.vector.tensor_copy(listed[:], table_scales[:].indirect(list_sb[:]))
             dealt = keep.tile([P, S], U8, name=name, align_bytes=64)
             nc.vector.tensor_copy(
                 dealt[:].bitcast(I32).rearrange("p (t h) -> p t h", t=PACK),
@@ -107,166 +126,154 @@ def tile_picked_ccmpmaxbhopmn_none_p_kernel(
         ca_words = gather_words(ca_sb, "ca_words", "ca_words")
         ca_scales = gather_scales(ca_sb, "ca_scales", "w_then_ca")
 
-        def product(lhs_words, lhs_scales, t, rhs_words, rhs_scales, dst, scale):
-            cols = slice(t * P, (t + 1) * P)
+        def product(lhs_words, lhs_scales, t, rhs_words, rhs_scales, dst, scale, pieces=(WHOLE,)):
             acc = psum.tile([P, S], F32, name="acc")
-            nc.tensor.matmul_mx(
-                out=acc[:],
-                lhsT=lhs_words[:, cols].bitcast(FP8X4),
-                lhsT_scale=lhs_scales[:, cols],
-                rhs=rhs_words[:].bitcast(FP8X4),
-                rhs_scale=rhs_scales[:],
-                start=True,
-                stop=True,
-            )
+            for cols in pieces:
+                nc.tensor.matmul_mx(
+                    out=acc[:, cols],
+                    lhsT=lhs_words[:, BLOCKS[t]].bitcast(FP8X4),
+                    lhsT_scale=lhs_scales[:, BLOCKS[t]],
+                    rhs=rhs_words[:, cols].bitcast(FP8X4),
+                    rhs_scale=rhs_scales[:, cols],
+                    start=True,
+                    stop=True,
+                )
             nc.scalar.activation(out=dst, in_=acc[:], func=COPY, scale=scale)
 
         for t in range(PACK):
-            product(w_words, w_scales, t, xq_words, xq_scales, first[t][:, :S], 1.0)
+            product(w_words, w_scales, t, xq_words, xq_scales, y_a[t][:, :S], 1.0)
 
         z_grouped = keep.tile([P, PACK * S], BF16, name="z_grouped", tag="z_then_cb", align_bytes=64)
         z_view = z_grouped[:].rearrange("p (c t) -> p c t", t=PACK)
-        hop2 = {}
+        last = PACK - 1
 
-        def fetch1(t):
-            nc.vector.tensor_copy(second[t][:, S:], first[t][:].indirect(n1_sb[:]))
+        def fetch_y(t):
+            nc.vector.tensor_copy(st_nb[t][:, S:], y_a[t][:].indirect(n1_sb[:]))
 
-        def larger(t):
-            nc.vector.tensor_tensor(second[t][:, :S], first[t][:, :S], second[t][:, S:], ALU.max)
+        def make_st(t):
+            nc.vector.tensor_tensor(st_nb[t][:, :S], y_a[t][:, :S], st_nb[t][:, S:], ALU.max)
 
-        def fetch2(t):
-            if t == PACK - 1:
-                hop2[t] = keep.tile([P, S], F32, name="hop2_last", tag="last_then_cb", align_bytes=64)
-            else:
-                hop2[t] = work.tile([P, S], F32, name="hop2")
-            nc.vector.tensor_copy(hop2[t][:], second[t][:].indirect(n2_sb[:]))
+        def fetch_st(t, st_n2, cols):
+            nc.vector.tensor_copy(st_n2[:, cols], st_nb[t][:].indirect(entries(n2_sb, cols)))
 
-        def smaller(t):
-            low = work.tile([P, S], F32, name="low")
-            nc.vector.tensor_tensor(low[:], second[t][:, :S], hop2[t][:], ALU.min)
-            nc.scalar.activation(out=z_view[:, :, t], in_=low[:], func=COPY, scale=gain[:, t : t + 1])
+        def make_z(t, st_n2, low, cols):
+            nc.vector.tensor_tensor(low[:, cols], st_nb[t][:, cols], st_n2[:, cols], ALU.min)
+            nc.scalar.activation(out=z_view[:, cols, t], in_=low[:, cols], func=COPY, scale=gain[:, t : t + 1])
 
-        fetch1(0)
-        fetch1(1)
-        larger(0)
-        larger(1)
-        fetch2(0)
-        fetch1(2)
-        smaller(0)
-        fetch2(1)
-        larger(2)
-        fetch1(3)
-        smaller(1)
-        fetch2(2)
-        larger(3)
-        smaller(2)
-        hop2_last = keep.tile([P, S], F32, name="hop2_last", tag="last_then_cb", align_bytes=64)
-        low_last = work.tile([P, S], F32, name="low")
-        halves = [slice(h * (S // 2), (h + 1) * (S // 2)) for h in range(2)]
-        for cols in halves:
-            nc.vector.tensor_copy(hop2_last[:, cols], second[3][:].indirect(n2_sb[:, cols.start // 16 : cols.stop // 16]))
-        for cols in halves:
-            nc.vector.tensor_tensor(low_last[:, cols], second[3][:, cols], hop2_last[:, cols], ALU.min)
-            nc.scalar.activation(out=z_view[:, cols, 3], in_=low_last[:, cols], func=COPY, scale=gain[:, 3:4])
+        for t in range(2):
+            fetch_y(t)
+        for t in range(2):
+            make_st(t)
+        for t in range(last):
+            st_n2 = work.tile([P, S], F32, name="st_n2")
+            fetch_st(t, st_n2, WHOLE)
+            if t > 0:
+                make_st(t + 1)
+            if t + 2 < PACK:
+                fetch_y(t + 2)
+            low = work.tile([P, S], F32, name="low", bufs=PACK)
+            make_z(t, st_n2, low, WHOLE)
+        st_n2_last = keep.tile([P, S], F32, name="st_n2_last", tag="last_then_cb", align_bytes=64)
+        low = work.tile([P, S], F32, name="low", bufs=PACK)
+        for cols in HALVES:
+            fetch_st(last, st_n2_last, cols)
+        for cols in HALVES:
+            make_z(last, st_n2_last, low, cols)
 
         cb_scales = gather_scales(cb_sb, "cb_scales", "last_then_cb")
         z_words = keep.tile([P, S], U32, name="z_words", align_bytes=64)
         z_scales = keep.tile([P, S], U8, name="z_scales", align_bytes=64)
-        nc.vector.quantize_mx(out=z_words[:].bitcast(FP8X4), scales=z_scales[:], in_=z_grouped[:])
+        for cols in HALVES:
+            quantize(z_words, z_scales, z_grouped, cols)
         cb_words = gather_words(cb_sb, "cb_words", "z_then_cb")
 
         out_rows = out.rearrange("(h t c) j -> t h c j", t=PACK, c=PACK)
         on_tensor, on_vector = (0, 1), (2, 3)
 
-        def score_a(t):
-            product(ca_words, ca_scales, t, z_words, z_scales, first[t][:, :S], 0.0625)
+        def score_a(t, pieces=(WHOLE,)):
+            product(ca_words, ca_scales, t, z_words, z_scales, y_a[t][:, :S], SCORE, pieces)
 
         def score_neg_b(t):
-            product(cb_words, cb_scales, t, z_words, z_scales, second[t][:, :S], -0.0625)
+            product(cb_words, cb_scales, t, z_words, z_scales, st_nb[t][:, :S], -SCORE)
 
-        score_a(2)
+        a_n3, nb_n4, neg_low, high = {}, {}, {}, {}
+
+        def fetch_a(t):
+            a_n3[t] = work.tile([P, S], F32, name="a_n3")
+            nc.vector.tensor_copy(a_n3[t][:], y_a[t][:].indirect(n3_sb[:]))
+
+        score_a(on_vector[0], HALVES)
+        score_a(on_vector[1])
         for t in on_tensor:
             score_a(t)
             score_neg_b(t)
-        score_neg_b(2)
-        score_a(3)
-        score_neg_b(3)
-
-        a3, neg_b4, neg_low, high = {}, {}, {}, {}
-
-        def fetch3(t):
-            a3[t] = work.tile([P, S], F32, name="a3")
-            nc.vector.tensor_copy(a3[t][:], first[t][:].indirect(n3_sb[:]))
-
-        fetch3(2)
+        for t in on_vector:
+            score_neg_b(t)
+        for t in on_vector:
+            fetch_a(t)
 
         excess = {}
         for t in on_tensor:
-            a, neg_b = first[t][:, :S], second[t][:, :S]
-            for side, (window, index_sb, other) in enumerate([(second[t], n4_sb, a), (first[t], n3_sb, neg_b)]):
-                diff = work.tile([P, S], F32, name="diff", bufs=4)
-                nc.vector.tensor_tensor(diff[:], window[:].indirect(index_sb[:]), other, ALU.add)
-                excess[t, side] = work.tile([P, S], F32, name="excess", bufs=4)
+            a, neg_b = y_a[t][:, :S], st_nb[t][:, :S]
+            for side, (window, list_sb, other) in enumerate([(st_nb[t], n4_sb, a), (y_a[t], n3_sb, neg_b)]):
+                diff = work.tile([P, S], F32, name="diff", bufs=2 * len(on_tensor))
+                nc.vector.tensor_tensor(diff[:], window[:].indirect(list_sb[:]), other, ALU.add)
+                excess[t, side] = work.tile([P, S], F32, name="excess", bufs=2 * len(on_tensor))
                 nc.scalar.activation(out=excess[t, side][:], in_=diff[:], func=RELU, scale=-1.0)
 
         turned_sb = {}
         for t in on_tensor:
             turned = psum_sum.tile([P, S], F32, name="turned")
-            addends = [first[t][:, :S], second[t][:, :S], excess[t, 0][:], excess[t, 1][:]]
-            for n, term in enumerate(addends):
-                for c in range(PACK):
-                    cols = slice(c * P, (c + 1) * P)
+            terms = [y_a[t][:, :S], st_nb[t][:, :S], excess[t, 0][:], excess[t, 1][:]]
+            for n, term in enumerate(terms):
+                for c, cols in enumerate(BLOCKS):
                     nc.tensor.matmul(
                         turned[:, cols],
                         term[:, cols],
                         identity[:],
                         is_transpose=True,
                         start=(n == 0 and c == 0),
-                        stop=(n == len(addends) - 1 and c == PACK - 1),
+                        stop=(n == len(terms) - 1 and c == PACK - 1),
                     )
             turned_sb[t] = work.tile([P, S], F32, name="turned_sb")
             nc.scalar.copy(out=turned_sb[t][:], in_=turned[:])
         for t in on_tensor:
             back = psum_sum.tile([P, S], F32, name="back")
-            for c in range(PACK):
-                cols = slice(c * P, (c + 1) * P)
+            for cols in BLOCKS:
                 nc.tensor.transpose(back[:, cols], turned_sb[t][:, cols], identity[:])
-            res = work.tile([P, S], F32, name="res", bufs=3)
-            nc.scalar.copy(out=res[:], in_=back[:])
-            nc.scalar.dma_start(out=out_rows[t], in_=res[:])
+            summed = work.tile([P, S], F32, name="summed")
+            nc.scalar.copy(out=summed[:], in_=back[:])
+            nc.scalar.dma_start(out=out_rows[t], in_=summed[:])
 
-        def fetch4(t, cols):
-            offsets = n4_sb[:, cols.start // 16 : cols.stop // 16]
-            nc.vector.tensor_copy(neg_b4[t][:, cols], second[t][:].indirect(offsets))
+        def fetch_nb(t, cols):
+            nc.vector.tensor_copy(nb_n4[t][:, cols], st_nb[t][:].indirect(entries(n4_sb, cols)))
 
-        def low_side(t):
-            nc.vector.scalar_tensor_tensor(neg_low[t][:], a3[t][:], -1.0, second[t][:, :S], ALU.mult, ALU.max)
+        def make_neg_low(t):
+            nc.vector.scalar_tensor_tensor(neg_low[t][:], a_n3[t][:], -1.0, st_nb[t][:, :S], ALU.mult, ALU.max)
 
-        def high_side(t, cols):
+        def make_high(t, cols):
             nc.vector.scalar_tensor_tensor(
-                high[t][:, cols], neg_b4[t][:, cols], -1.0, first[t][:, cols], ALU.mult, ALU.max
+                high[t][:, cols], nb_n4[t][:, cols], -1.0, y_a[t][:, cols], ALU.mult, ALU.max
             )
 
         def finish(t, cols):
-            res = work.tile([P, cols.stop - cols.start], F32, name="res_v", bufs=3)
+            res = work.tile([P, cols.stop - cols.start], F32, name="res", bufs=3)
             nc.vector.tensor_tensor(res[:], high[t][:, cols], neg_low[t][:, cols], ALU.add)
             nc.sync.dma_start(out=out_rows[t][:, :, cols], in_=res[:])
 
         for t in on_vector:
-            neg_b4[t] = work.tile([P, S], F32, name="neg_b4")
+            nb_n4[t] = work.tile([P, S], F32, name="nb_n4")
             neg_low[t] = work.tile([P, S], F32, name="neg_low")
             high[t] = work.tile([P, S], F32, name="high")
-        whole = slice(0, S)
-        halves = [slice(h * (S // 2), (h + 1) * (S // 2)) for h in range(2)]
-        fetch4(2, whole)
-        low_side(2)
-        high_side(2, whole)
-        fetch3(3)
-        finish(2, whole)
-        fetch4(3, halves[0])
-        low_side(3)
-        fetch4(3, halves[1])
-        for cols in halves:
-            high_side(3, cols)
-        for cols in halves:
-            finish(3, cols)
+        before, final = on_vector
+        fetch_nb(before, WHOLE)
+        make_neg_low(before)
+        make_high(before, WHOLE)
+        fetch_nb(final, HALVES[0])
+        finish(before, WHOLE)
+        fetch_nb(final, HALVES[1])
+        make_neg_low(final)
+        for cols in HALVES:
+            make_high(final, cols)
+        for cols in HALVES:
+            finish(final, cols)

from contextlib import ExitStack

import concourse.mybir as mybir
from concourse.masks import make_identity

K, T, S = 512, 2048, 512
P = 128
PACK = 4
LIST_ROWS = 16
SCORE = 0.0625
FLOPS = 3 * 2 * K * S * S

F32 = mybir.dt.float32
BF16 = mybir.dt.bfloat16
I32 = mybir.dt.int32
U32 = mybir.dt.uint32
U16 = mybir.dt.uint16
U8 = mybir.dt.uint8
FP8X4 = mybir.dt.float8_e4m3fn_x4
ALU = mybir.AluOpType
COPY = mybir.ActivationFunctionType.Copy
RELU = mybir.ActivationFunctionType.Relu

WHOLE = slice(0, S)
HALVES = (slice(0, S // 2), slice(S // 2, S))
BLOCKS = tuple(slice(c * P, (c + 1) * P) for c in range(PACK))


def entries(list_sb, cols):
    return list_sb[:, cols.start // LIST_ROWS : cols.stop // LIST_ROWS]


def tile_picked_ccmpmaxbhopmn_none_p_kernel(
    tc, x_words, x_scales, w1, gs, offs, n1, n2, ca, cb, n3, n4, out
):
    nc = tc.nc
    with ExitStack() as ctx:
        lists = ctx.enter_context(tc.tile_pool(name="lists", bufs=1))
        keep = ctx.enter_context(tc.tile_pool(name="keep", bufs=1))
        work = ctx.enter_context(tc.tile_pool(name="work", bufs=2))
        psum = ctx.enter_context(tc.psum_pool(name="psum", bufs=4))
        psum_sum = ctx.enter_context(tc.psum_pool(name="psum_sum", bufs=2))

        table_scales = keep.tile([P, T], U8, name="table_scales", align_bytes=64)
        nc.vector.memset(table_scales[:].bitcast(I32), 0)

        table_words = keep.tile([P, T], I32, name="table_words", align_bytes=64)
        nc.scalar.dma_start(out=table_words[:], in_=x_words[0].rearrange("p n t -> p (n t)").bitcast(I32))

        def load_list(src, name):
            dst = lists.tile([P, S // LIST_ROWS], U16, name=name)
            nc.sync.dma_start(dst[:], src)
            return dst

        offs_sb = load_list(offs, "offs_sb")
        ca_sb = load_list(ca, "ca_sb")
        for q in range(4):
            nc.sync.dma_start(
                out=table_scales[32 * q : 32 * q + 4, :].bitcast(I32),
                in_=x_scales[0, 4 * q : 4 * q + 4, :].bitcast(I32),
            )
        w_rows = w1.rearrange("(p j) c -> p j c", j=PACK)
        w_raw = []
        for h, cols in enumerate(HALVES):
            half = keep.tile([P, PACK, S // 2], F32, name=f"w_raw{h}")
            nc.scalar.dma_start(out=half[:], in_=w_rows[:, :, cols])
            w_raw.append(half)
        n1_sb = load_list(n1, "n1_sb")
        n2_sb = load_list(n2, "n2_sb")
        gain = keep.tile([P, PACK], F32, name="gain")
        nc.gpsimd.dma_start(out=gain[:], in_=gs.rearrange("(p t) o -> p (t o)", t=PACK))
        cb_sb = load_list(cb, "cb_sb")
        n3_sb = load_list(n3, "n3_sb")
        n4_sb = load_list(n4, "n4_sb")

        y_a = [keep.tile([P, 2 * S], F32, name=f"y_a{t}") for t in range(PACK)]
        st_nb = [keep.tile([P, 2 * S], F32, name=f"st_nb{t}") for t in range(PACK)]
        for t in range(PACK):
            nc.vector.memset(y_a[t][:, S:], 0.0)

        identity = keep.tile([P, P], F32, name="identity")
        make_identity(nc, identity[:])

        words_window = table_words[:].bitcast(U32)
        xq_words = keep.tile([P, S], U32, name="xq_words", align_bytes=64)
        xq_scales = keep.tile([P, S], U8, name="xq_scales", align_bytes=64)
        nc.vector.tensor_copy(xq_words[:], words_window.indirect(offs_sb[:]))
        nc.vector.tensor_copy(xq_scales[:], table_scales[:].indirect(offs_sb[:]))

        w_grouped = keep.tile([P, PACK * S], BF16, name="w_grouped", tag="w_then_ca", align_bytes=64)
        w_view = w_grouped[:].rearrange("p (t m j) -> p m j t", t=PACK, j=PACK)
        for h in range(2):
            nc.scalar.copy(
                out=w_view[:, h * (P // 2) : (h + 1) * (P // 2), :, :],
                in_=w_raw[h][:].rearrange("p j (m t) -> p m j t", t=PACK),
            )

        def quantize(words, scales, grouped, cols):
            nc.vector.quantize_mx(
                out=words[:, cols].bitcast(FP8X4),
                scales=scales[:, cols],
                in_=grouped[:, PACK * cols.start : PACK * cols.stop],
            )

        w_words = keep.tile([P, S], U32, name="w_words", align_bytes=64)
        w_scales = keep.tile([P, S], U8, name="w_scales", align_bytes=64)
        for cols in BLOCKS:
            quantize(w_words, w_scales, w_grouped, cols)

        def gather_words(list_sb, name, tag):
            words = keep.tile([P, S], U32, name=name, tag=tag, align_bytes=64)
            dealt_view = words[:].rearrange("p (t h c) -> p h t c", t=PACK, c=PACK)
            nc.vector.tensor_copy(dealt_view, words_window.indirect(list_sb[:]))
            return words

        def gather_scales(list_sb, name, tag):
            listed = keep.tile([P, S], U8, name=name + "_listed", tag=tag, align_bytes=64)
            nc.vector.tensor_copy(listed[:], table_scales[:].indirect(list_sb[:]))
            dealt = keep.tile([P, S], U8, name=name, align_bytes=64)
            nc.vector.tensor_copy(
                dealt[:].bitcast(I32).rearrange("p (t h) -> p t h", t=PACK),
                listed[:].bitcast(I32).rearrange("p (h t) -> p t h", t=PACK),
            )
            return dealt

        ca_words = gather_words(ca_sb, "ca_words", "ca_words")
        ca_scales = gather_scales(ca_sb, "ca_scales", "w_then_ca")

        def product(lhs_words, lhs_scales, t, rhs_words, rhs_scales, dst, scale, pieces=(WHOLE,)):
            acc = psum.tile([P, S], F32, name="acc")
            for cols in pieces:
                nc.tensor.matmul_mx(
                    out=acc[:, cols],
                    lhsT=lhs_words[:, BLOCKS[t]].bitcast(FP8X4),
                    lhsT_scale=lhs_scales[:, BLOCKS[t]],
                    rhs=rhs_words[:, cols].bitcast(FP8X4),
                    rhs_scale=rhs_scales[:, cols],
                    start=True,
                    stop=True,
                )
            nc.scalar.activation(out=dst, in_=acc[:], func=COPY, scale=scale)

        for t in range(PACK):
            product(w_words, w_scales, t, xq_words, xq_scales, y_a[t][:, :S], 1.0)

        z_grouped = keep.tile([P, PACK * S], BF16, name="z_grouped", tag="z_then_cb", align_bytes=64)
        z_view = z_grouped[:].rearrange("p (c t) -> p c t", t=PACK)
        last = PACK - 1

        def fetch_y(t):
            nc.vector.tensor_copy(st_nb[t][:, S:], y_a[t][:].indirect(n1_sb[:]))

        def make_st(t):
            nc.vector.tensor_tensor(st_nb[t][:, :S], y_a[t][:, :S], st_nb[t][:, S:], ALU.max)

        def fetch_st(t, st_n2, cols):
            nc.vector.tensor_copy(st_n2[:, cols], st_nb[t][:].indirect(entries(n2_sb, cols)))

        def make_z(t, st_n2, low, cols):
            nc.vector.tensor_tensor(low[:, cols], st_nb[t][:, cols], st_n2[:, cols], ALU.min)
            nc.scalar.activation(out=z_view[:, cols, t], in_=low[:, cols], func=COPY, scale=gain[:, t : t + 1])

        for t in range(2):
            fetch_y(t)
        for t in range(2):
            make_st(t)
        for t in range(last):
            st_n2 = work.tile([P, S], F32, name="st_n2")
            fetch_st(t, st_n2, WHOLE)
            if t > 0:
                make_st(t + 1)
            if t + 2 < PACK:
                fetch_y(t + 2)
            low = work.tile([P, S], F32, name="low", bufs=PACK)
            make_z(t, st_n2, low, WHOLE)
        st_n2_last = keep.tile([P, S], F32, name="st_n2_last", tag="last_then_cb", align_bytes=64)
        low = work.tile([P, S], F32, name="low", bufs=PACK)
        for cols in HALVES:
            fetch_st(last, st_n2_last, cols)
        for cols in HALVES:
            make_z(last, st_n2_last, low, cols)

        cb_scales = gather_scales(cb_sb, "cb_scales", "last_then_cb")
        z_words = keep.tile([P, S], U32, name="z_words", align_bytes=64)
        z_scales = keep.tile([P, S], U8, name="z_scales", align_bytes=64)
        for cols in HALVES:
            quantize(z_words, z_scales, z_grouped, cols)
        cb_words = gather_words(cb_sb, "cb_words", "z_then_cb")

        out_rows = out.rearrange("(h t c) j -> t h c j", t=PACK, c=PACK)
        on_tensor, on_vector = (0, 1), (2, 3)

        def score_a(t, pieces=(WHOLE,)):
            product(ca_words, ca_scales, t, z_words, z_scales, y_a[t][:, :S], SCORE, pieces)

        def score_neg_b(t):
            product(cb_words, cb_scales, t, z_words, z_scales, st_nb[t][:, :S], -SCORE)

        a_n3, nb_n4, neg_low, high = {}, {}, {}, {}

        def fetch_a(t):
            a_n3[t] = work.tile([P, S], F32, name="a_n3")
            nc.vector.tensor_copy(a_n3[t][:], y_a[t][:].indirect(n3_sb[:]))

        score_a(on_vector[0], HALVES)
        score_a(on_vector[1])
        for t in on_tensor:
            score_a(t)
            score_neg_b(t)
        for t in on_vector:
            score_neg_b(t)
        for t in on_vector:
            fetch_a(t)

        excess = {}
        for t in on_tensor:
            a, neg_b = y_a[t][:, :S], st_nb[t][:, :S]
            for side, (window, list_sb, other) in enumerate([(st_nb[t], n4_sb, a), (y_a[t], n3_sb, neg_b)]):
                diff = work.tile([P, S], F32, name="diff", bufs=2 * len(on_tensor))
                nc.vector.tensor_tensor(diff[:], window[:].indirect(list_sb[:]), other, ALU.add)
                excess[t, side] = work.tile([P, S], F32, name="excess", bufs=2 * len(on_tensor))
                nc.scalar.activation(out=excess[t, side][:], in_=diff[:], func=RELU, scale=-1.0)

        turned_sb = {}
        for t in on_tensor:
            turned = psum_sum.tile([P, S], F32, name="turned")
            terms = [y_a[t][:, :S], st_nb[t][:, :S], excess[t, 0][:], excess[t, 1][:]]
            for n, term in enumerate(terms):
                for c, cols in enumerate(BLOCKS):
                    nc.tensor.matmul(
                        turned[:, cols],
                        term[:, cols],
                        identity[:],
                        is_transpose=True,
                        start=(n == 0 and c == 0),
                        stop=(n == len(terms) - 1 and c == PACK - 1),
                    )
            turned_sb[t] = work.tile([P, S], F32, name="turned_sb")
            nc.scalar.copy(out=turned_sb[t][:], in_=turned[:])
        for t in on_tensor:
            back = psum_sum.tile([P, S], F32, name="back")
            for cols in BLOCKS:
                nc.tensor.transpose(back[:, cols], turned_sb[t][:, cols], identity[:])
            summed = work.tile([P, S], F32, name="summed")
            nc.scalar.copy(out=summed[:], in_=back[:])
            nc.scalar.dma_start(out=out_rows[t], in_=summed[:])

        def fetch_nb(t, cols):
            nc.vector.tensor_copy(nb_n4[t][:, cols], st_nb[t][:].indirect(entries(n4_sb, cols)))

        def make_neg_low(t):
            nc.vector.scalar_tensor_tensor(neg_low[t][:], a_n3[t][:], -1.0, st_nb[t][:, :S], ALU.mult, ALU.max)

        def make_high(t, cols):
            nc.vector.scalar_tensor_tensor(
                high[t][:, cols], nb_n4[t][:, cols], -1.0, y_a[t][:, cols], ALU.mult, ALU.max
            )

        def finish(t, cols):
            res = work.tile([P, cols.stop - cols.start], F32, name="res", bufs=3)
            nc.vector.tensor_tensor(res[:], high[t][:, cols], neg_low[t][:, cols], ALU.add)
            nc.sync.dma_start(out=out_rows[t][:, :, cols], in_=res[:])

        for t in on_vector:
            nb_n4[t] = work.tile([P, S], F32, name="nb_n4")
            neg_low[t] = work.tile([P, S], F32, name="neg_low")
            high[t] = work.tile([P, S], F32, name="high")
        before, final = on_vector
        fetch_nb(before, WHOLE)
        make_neg_low(before)
        make_high(before, WHOLE)
        fetch_nb(final, HALVES[0])
        finish(before, WHOLE)
        fetch_nb(final, HALVES[1])
        make_neg_low(final)
        for cols in HALVES:
            make_high(final, cols)
        for cols in HALVES:
            finish(final, cols)
